import numpy as np
import ml_dtypes


def mxq(x, axis, fmt="e4m3"):
    dtype, down = {"e4m3": (ml_dtypes.float8_e4m3fn, 7), "e5m2": (ml_dtypes.float8_e5m2, 14)}[fmt]
    v = np.moveaxis(np.asarray(x, np.float32).astype(ml_dtypes.bfloat16).astype(np.float64), axis, -1)
    blocks = v.reshape(v.shape[:-1] + (-1, 32))
    amax = np.abs(blocks).max(-1, keepdims=True)
    byte = np.maximum(np.where(amax > 0, np.frexp(amax)[1] - 1 + 127, 0) - down, 1)
    scale = np.exp2(byte - 127.0)
    codes = (blocks / scale).astype(np.float32).astype(dtype).astype(np.float64)
    return np.moveaxis((codes * scale).reshape(v.shape), -1, axis)


WIDE = False


def mx_kscale(k):
    if not WIDE:
        return np.ones(k)
    levels = np.array([10, -10, 5, -5, 0])
    if k % 512:
        return np.exp2(np.random.permutation(np.resize(levels, k // 32))).repeat(32)
    a = np.empty((k // 512, 16))
    for p in range(k // 512):
        a[p, :8] = np.random.permutation(np.resize(levels, 8))
        for g in range(8):
            far = levels[np.abs(levels - a[p, g]) >= 10]
            a[p, g + 8] = far[np.random.randint(len(far))]
    return np.exp2(a.ravel()).repeat(32)


def f64(x):
    return np.asarray(x).astype(np.float64)


def striped(idx):
    return np.tile(np.asarray(idx).reshape(-1, 16).T, (8, 1)).astype(np.uint16)


def unstriped(offs):
    return offs[:16].T.reshape(-1).astype(np.int64)


E2M1 = np.array([0.0, 0.5, 1.0, 1.5, 2.0, 3.0, 4.0, 6.0, -0.0, -0.5, -1.0, -1.5, -2.0, -3.0, -4.0, -6.0])


def pack_weight(w, fmt):
    k, n = w.shape
    w = f64(np.asarray(w, np.float32).astype(ml_dtypes.bfloat16)).reshape(k // 32, 32, n)
    amax = np.abs(w).max(1)
    if fmt == "e4m3":
        byte = np.frexp(amax)[1] - 1 + 127 - 7
    else:
        mant, ex = np.frexp(amax / 6.0)
        byte = np.where(mant > 0.5, ex, ex - 1) + 127
    byte = np.clip(np.where(amax > 0, byte, 1), 1, 254)
    scaled = (w * np.exp2(127.0 - byte)[:, None, :]).reshape(k, n).astype(np.float32)
    by_word = np.ascontiguousarray(scaled.reshape(k // 512, 128, 4, n).transpose(0, 1, 3, 2))
    if fmt == "e4m3":
        words = by_word.astype(ml_dtypes.float8_e4m3fn).view(np.uint8)
    else:
        c = by_word.astype(ml_dtypes.float4_e2m1fn).view(np.uint8) & 0xF
        words = (c[..., 0::2] | (c[..., 1::2] << 4)).reshape(k // 512, 128, 2 * n)
    return np.ascontiguousarray(words), np.ascontiguousarray(byte.astype(np.uint8).reshape(k // 512, 16, n))


def unpack_weight(words, scales, fmt):
    g, _, n = scales.shape
    words = np.ascontiguousarray(words).reshape(g, 128, n, -1)
    if fmt == "e4m3":
        vals = words.view(ml_dtypes.float8_e4m3fn).astype(np.float64)
    else:
        nib = np.empty((g, 128, n, 4), np.uint8)
        nib[..., 0::2] = words & 0xF
        nib[..., 1::2] = words >> 4
        vals = E2M1[nib]
    vals = vals * np.repeat(np.exp2(scales.astype(np.float64) - 127.0), 8, axis=1)[..., None]
    return vals.transpose(0, 1, 3, 2).reshape(g * 512, n)


def silu(v):
    return v / (1.0 + np.exp(-v))


B, N, T, D, NQ = 1, 512, 2048, 1024, 512
DV = 512


def sgn(shape):
    return np.random.uniform(0.5, 2.0, shape) * np.where(np.random.standard_normal(shape) < 0, -1.0, 1.0)


def setup_inputs():
    n = np.random.standard_normal
    pages = np.random.permutation(T // 64)[:B * N // 64]
    idx = (pages[:, None] * 64 + np.arange(64)[None, :]).reshape(-1)
    s = mx_kscale(D)[:, None]
    u = mx_kscale(N)
    ut = np.ones(T)
    ut[idx] = u
    kp = pack_weight(n((D, T)) / s, "e2m1")
    return {
        "qT": (n((B, D, NQ)) * s * (1.00 / np.sqrt(D))).astype(np.float32),
        "k_words": np.ascontiguousarray(kp[0].reshape(1, 2, 128, T, 2).transpose(0, 2, 3, 1, 4)).reshape(1, 128, T, 4),
        "k_scales": kp[1],
        "vT": (n((DV, T)) / ut).astype(np.float32),
        "nb": np.tile(0.5 * n(2048), (128, 1)).astype(np.float32),
        "us": (sgn((B, N, 1)) * u[:, None]).astype(np.float32),
        "offs": striped(idx),
    }


def reference(qT, k_words, k_scales, vT, nb, us, offs):
    idx = unstriped(offs)
    pick = lambda x, which: x[:, which].reshape(x.shape[0], B, -1).transpose(1, 0, 2)
    k = unpack_weight(k_words.reshape(1, 128, T, 2, 2).transpose(0, 3, 1, 2, 4).reshape(2, 128, 2 * T), k_scales, "e2m1")
    kg = pick(k, idx)
    qq = mxq(f64(qT), 1, "e4m3")
    a = kg.transpose(0, 2, 1) @ qq
    y = silu(a + pick(f64(nb), idx)[:, :1, :].transpose(0, 2, 1)) * f64(us)
    wq = mxq(y, 1, "e4m3")
    o = wq.transpose(0, 2, 1) @ mxq(pick(f64(vT), idx).transpose(0, 2, 1), 1, "e4m3")
    return o

@@ -1,0 +1,209 @@
+from contextlib import ExitStack
+
+import concourse.mybir as mybir
+from concourse.masks import make_identity
+
+N, T, D, NQ, DV = 512, 2048, 1024, 512, 512
+FLOPS = 2 * N * NQ * D + 2 * N * NQ * DV
+BYTES = 4 * D * NQ + 128 * T * 4 + 32 * T + 4 * DV * T + 4 * T + 4 * N + 128 * (N // 16) * 2 + 4 * NQ * DV
+
+F32 = mybir.dt.float32
+BF16 = mybir.dt.bfloat16
+I32 = mybir.dt.int32
+U32 = mybir.dt.uint32
+U16 = mybir.dt.uint16
+U8 = mybir.dt.uint8
+FP8X4 = mybir.dt.float8_e4m3fn_x4
+FP4X4 = mybir.dt.float4_e2m1fn_x4
+SILU = mybir.ActivationFunctionType.Silu
+MULT = mybir.AluOpType.mult
+
+P = 128
+PACK = 4
+
+
+def tile_attend_mlpb_silu_kernel(tc, qT, k_words, k_scales, vT, nb, us, offs, out):
+    nc = tc.nc
+    with ExitStack() as ctx:
+        keep = ctx.enter_context(tc.tile_pool(name="keep", bufs=1))
+        big = ctx.enter_context(tc.tile_pool(name="big", bufs=1))
+        ring = ctx.enter_context(tc.tile_pool(name="ring", bufs=2))
+        psum = ctx.enter_context(tc.psum_pool(name="psum", bufs=1))
+
+        offsets = keep.tile([P, N // 16], U16, name="offsets")
+        nc.sync.dma_start(offsets[:], offs)
+
+        ks_win = keep.tile([P, T], U8, name="ks_win", align_bytes=64)
+        nb_win = keep.tile([P, T], F32, name="nb_win", align_bytes=64)
+        ks_plane1 = keep.tile([P, N], U8, name="ks_plane1", align_bytes=64)
+        nc.vector.memset(ks_win[:].bitcast(I32), 0)
+        nc.vector.memset(nb_win[:], 0.0)
+        nc.vector.memset(ks_plane1[:].bitcast(I32), 0)
+        ident = keep.tile([P, P], F32, name="ident")
+        make_identity(nc, ident[:])
+
+        def load_q(o):
+            raw = big.tile([P, PACK, NQ], F32, name="q_raw", tag="slot_" + "ca"[o], align_bytes=64)
+            nc.sync.dma_start(raw[:], qT[0, 512 * o : 512 * (o + 1), :].rearrange("(p j) w -> p j w", j=PACK))
+            return raw
+
+        us_col = keep.tile([P, PACK], F32, name="us_col")
+        nc.sync.dma_start(us_col[:], us[0].rearrange("(p r) o -> p (r o)", r=PACK))
+        kw_win = big.tile([P, T], U32, name="kw_win", tag="slot_a", align_bytes=64)
+        nc.sync.dma_start(kw_win[:].bitcast(I32), k_words[0].rearrange("p t b -> p (t b)").bitcast(I32))
+
+        q_raw0 = load_q(0)
+        for quad in range(4):
+            nc.scalar.dma_start(
+                ks_win[32 * quad : 32 * quad + 8, :].bitcast(I32),
+                k_scales[:, 4 * quad : 4 * quad + 4, :].bitcast(I32),
+            )
+        nc.scalar.dma_start(nb_win[0:1, :], nb[0:1, :])
+
+        warm = keep.tile([P, 1], F32, name="warm")
+        nc.scalar.activation(warm[:], us_col[:, 0:1], SILU)
+
+        q_codes = keep.tile([P, 2, NQ], U32, name="q_codes", align_bytes=64)
+        q_scales = keep.tile([P, 2, NQ], U8, name="q_scales", align_bytes=64)
+
+        def weave(copy, dst, src, c0, c1):
+            copy(
+                dst[:].rearrange("p (c i) t -> p c t i", i=4),
+                src[:, :, c0:c1].rearrange("p t (c i) -> p c t i", i=4),
+            )
+
+        def quant(codes, scales, grouped, c0, c1):
+            nc.vector.quantize_mx(
+                out=codes[:, c0:c1].bitcast(FP8X4),
+                scales=scales[:, c0:c1],
+                in_=grouped[:].rearrange("p w j -> p (w j)"),
+            )
+
+        kw_got = keep.tile([P, N], U32, name="kw_got", align_bytes=64)
+        nc.vector.tensor_copy(kw_got[:], kw_win[:].indirect(offsets[:]))
+        q_raw1 = load_q(1)
+        ks_got = big.tile([P, N], U8, name="ks_got", tag="slot_b", align_bytes=64)
+        nc.vector.tensor_copy(ks_got[:], ks_win[:].indirect(offsets[:]))
+        ks_dealt = keep.tile([P, N], U8, name="ks_dealt", align_bytes=64)
+        nc.vector.tensor_copy(
+            ks_dealt[:].rearrange("p (r s) -> p s r", r=PACK),
+            ks_got[:].rearrange("p (s r) -> p s r", r=PACK),
+        )
+        nc.sync.dma_start(ks_plane1[0:112, :].bitcast(I32), ks_dealt[4:116, :].bitcast(I32))
+        ks_planes = [ks_dealt, ks_plane1]
+        kw_dealt = keep.tile([P, 2, N], U16, name="kw_dealt", align_bytes=64)
+        kw_half = kw_got[:].bitcast(U16).rearrange("p (s r o) -> p o s r", r=PACK, o=2)
+        for o in range(2):
+            nc.vector.tensor_copy(kw_dealt[:, o, :].rearrange("p (r s) -> p s r", r=PACK), kw_half[:, o, :, :])
+
+        q_grp0 = big.tile([P, NQ, PACK], BF16, name="q_grp0", tag="slot_d", align_bytes=64)
+        weave(nc.scalar.copy, q_grp0, q_raw0, 0, NQ)
+        quant(q_codes[:, 0, :], q_scales[:, 0, :], q_grp0, 0, NQ)
+
+        nb_got = keep.tile([P, N], F32, name="nb_got", align_bytes=64)
+        nc.vector.tensor_copy(nb_got[:], nb_win[:].indirect(offsets[:]))
+
+        banks = [psum.tile([P, NQ], F32, name=f"a{r}", tag=f"bank{r}") for r in range(PACK)]
+
+        def first_layer(o, r):
+            cols = slice(P * r, P * (r + 1))
+            nc.tensor.matmul_mx(
+                out=banks[r][:],
+                lhsT=kw_dealt[:, o, cols].bitcast(FP4X4),
+                lhsT_scale=ks_planes[o][:, cols],
+                rhs=q_codes[:, o, :].bitcast(FP8X4),
+                rhs_scale=q_scales[:, o, :],
+                start=(o == 0),
+                stop=(o == 1),
+            )
+
+        for r in range(PACK):
+            first_layer(0, r)
+
+        v_win = []
+        for c in range(4):
+            win = big.tile([P, T], F32, name="v_win", tag="slot_" + "bcda"[c], align_bytes=64)
+            nc.sync.dma_start(win[:], vT[P * c : P * (c + 1), :])
+            v_win.append(win)
+
+        q_grp1 = [keep.tile([P, 256, PACK], BF16, name=f"q_grp1_{h}", tag=f"q_grp1_{h}", align_bytes=64) for h in range(2)]
+        weave(nc.vector.tensor_copy, q_grp1[0], q_raw1, 0, 256)
+        weave(nc.scalar.copy, q_grp1[1], q_raw1, 256, NQ)
+        nb_ps = psum.tile([P, PACK, P], F32, name="nb_ps", tag="bank4")
+        nb_by_place = nb_got[:].rearrange("p (s r) -> p r s", r=PACK)
+        for r in range(PACK):
+            nc.tensor.transpose(nb_ps[:, r, :], nb_by_place[:, r, :], ident[:])
+        bias = keep.tile([P, PACK], F32, name="bias")
+        nc.scalar.copy(bias[:], nb_ps[:, :, 0])
+
+        quant(q_codes[:, 1, :], q_scales[:, 1, :], q_grp1[0], 0, 256)
+        quant(q_codes[:, 1, :], q_scales[:, 1, :], q_grp1[1], 256, NQ)
+        for r in range(PACK):
+            first_layer(1, r)
+
+        v_codes = keep.tile([P, DV], U32, name="v_codes", align_bytes=64)
+        v_scales = keep.tile([P, DV], U8, name="v_scales", align_bytes=64)
+
+        def gather_v(c, tag):
+            got = keep.tile([P, N], BF16, name="v_got", tag=tag, align_bytes=64)
+            nc.vector.tensor_copy(got[:], v_win[c][:].indirect(offsets[:]))
+            words = got[:].bitcast(F32).rearrange("p (s u) -> p u s", u=2)
+            turned = psum.tile([P, 2, P], F32, name="turned", tag=f"bank{5 + c % 2}")
+            for u in range(2):
+                nc.tensor.transpose(turned[:, u, :], words[:, u, :], ident[:])
+            grp = ring.tile([P, P, PACK], BF16, name="v_grp", align_bytes=64)
+            nc.scalar.copy(
+                grp[:].rearrange("p e j -> p (e j)").bitcast(F32).rearrange("p (e u) -> p e u", u=2),
+                turned[:].rearrange("p u e -> p e u"),
+            )
+            return grp
+
+        def quant_v(c, grp):
+            quant(v_codes[:], v_scales[:], grp, P * c, P * (c + 1))
+
+        act = [keep.tile([P, NQ], F32, name=f"act{r}", tag=f"act{r}", align_bytes=64) for r in range(PACK)]
+        y_rows = keep.tile([P, PACK, NQ], BF16, name="y_rows", align_bytes=64)
+        grp0 = gather_v(0, "q_grp1_1")
+        for r in range(PACK):
+            nc.scalar.activation(act[r][:], banks[r][:], SILU, bias=bias[:, r : r + 1])
+            nc.vector.tensor_scalar(y_rows[:, r, :], act[r][:], us_col[:, r : r + 1], None, MULT)
+        quant_v(0, grp0)
+        grp1 = gather_v(1, "act1")
+
+        y_grp = [keep.tile([P, 256, PACK], BF16, name=f"y_grp{h}", tag=f"y_grp{h}", align_bytes=64) for h in range(2)]
+        y_codes = keep.tile([P, NQ], U32, name="y_codes", align_bytes=64)
+        y_scales = keep.tile([P, NQ], U8, name="y_scales", align_bytes=64)
+        weave(nc.vector.tensor_copy, y_grp[0], y_rows, 0, 256)
+        weave(nc.scalar.copy, y_grp[1], y_rows, 256, NQ)
+        quant_v(1, grp1)
+        quant(y_codes[:], y_scales[:], y_grp[0], 0, 256)
+        quant(y_codes[:], y_scales[:], y_grp[1], 256, NQ)
+
+        out_rows = out[0].rearrange("(j p) e -> p j e", p=P)
+
+        def second_layer(e0, width, j0, nj, tag, copy):
+            acc = psum.tile([P, nj, width], F32, name="acc", tag=tag)
+            for j in range(nj):
+                rows = slice(P * (j0 + j), P * (j0 + j + 1))
+                nc.tensor.matmul_mx(
+                    out=acc[:, j, :],
+                    lhsT=y_codes[:, rows].bitcast(FP8X4),
+                    lhsT_scale=y_scales[:, rows],
+                    rhs=v_codes[:, e0 : e0 + width].bitcast(FP8X4),
+                    rhs_scale=v_scales[:, e0 : e0 + width],
+                    start=True,
+                    stop=True,
+                )
+            res = keep.tile([P, nj, width], F32, name=f"res_{e0}_{j0}")
+            copy(res[:], acc[:])
+            nc.sync.dma_start(out_rows[:, j0 : j0 + nj, e0 : e0 + width], res[:])
+
+        grp2 = gather_v(2, "y_grp0")
+        second_layer(0, 256, 0, 2, "bank0", nc.scalar.copy)
+        second_layer(0, 256, 2, 2, "bank1", nc.scalar.copy)
+        quant_v(2, grp2)
+        second_layer(256, 128, 0, 4, "bank2", nc.scalar.copy)
+        grp3 = gather_v(3, "y_grp1")
+        quant_v(3, grp3)
+        second_layer(384, 128, 0, 2, "bank3", nc.scalar.copy)
+        second_layer(384, 128, 2, 2, "bank7", nc.vector.tensor_copy)

@@ -16,10 +16,12 @@ U8 = mybir.dt.uint8
 FP8X4 = mybir.dt.float8_e4m3fn_x4
 FP4X4 = mybir.dt.float4_e2m1fn_x4
 SILU = mybir.ActivationFunctionType.Silu
+COPY = mybir.ActivationFunctionType.Copy
 MULT = mybir.AluOpType.mult
 
 P = 128
 PACK = 4
+SLOT = 4 * T
 
 
 def tile_attend_mlpb_silu_kernel(tc, qT, k_words, k_scales, vT, nb, us, offs, out):
@@ -27,43 +29,46 @@ def tile_attend_mlpb_silu_kernel(tc, qT, k_words, k_scales, vT, nb, us, offs, ou
     with ExitStack() as ctx:
         keep = ctx.enter_context(tc.tile_pool(name="keep", bufs=1))
         big = ctx.enter_context(tc.tile_pool(name="big", bufs=1))
-        ring = ctx.enter_context(tc.tile_pool(name="ring", bufs=2))
         psum = ctx.enter_context(tc.psum_pool(name="psum", bufs=1))
 
         offsets = keep.tile([P, N // 16], U16, name="offsets")
         nc.sync.dma_start(offsets[:], offs)
 
-        ks_win = keep.tile([P, T], U8, name="ks_win", align_bytes=64)
-        nb_win = keep.tile([P, T], F32, name="nb_win", align_bytes=64)
+        ks_win = keep.tile([P, T], U8, name="ks_win", tag="ks_win", align_bytes=64)
+        nb_win = keep.tile([P, T], F32, name="nb_win", tag="nb_win", align_bytes=64)
         ks_plane1 = keep.tile([P, N], U8, name="ks_plane1", align_bytes=64)
         nc.vector.memset(ks_win[:].bitcast(I32), 0)
         nc.vector.memset(nb_win[:], 0.0)
+        warm_in = keep.tile([P, 1], F32, name="warm_in")
+        nc.vector.memset(warm_in[:], 0.0)
         nc.vector.memset(ks_plane1[:].bitcast(I32), 0)
         ident = keep.tile([P, P], F32, name="ident")
         make_identity(nc, ident[:])
 
         def load_q(o):
-            raw = big.tile([P, PACK, NQ], F32, name="q_raw", tag="slot_" + "ca"[o], align_bytes=64)
+            raw = big.tile([P, PACK, NQ], F32, name=f"q_raw{o}", offset=(1 + o) * SLOT, align_bytes=64)
             nc.sync.dma_start(raw[:], qT[0, 512 * o : 512 * (o + 1), :].rearrange("(p j) w -> p j w", j=PACK))
             return raw
 
-        us_col = keep.tile([P, PACK], F32, name="us_col")
-        nc.sync.dma_start(us_col[:], us[0].rearrange("(p r) o -> p (r o)", r=PACK))
-        kw_win = big.tile([P, T], U32, name="kw_win", tag="slot_a", align_bytes=64)
+        us_stage = big.tile([P, 2 * T], F32, name="us_stage", offset=2 * SLOT, align_bytes=64)
+        nc.sync.dma_start(us_stage[:, 0:PACK], us[0].rearrange("(p r) o -> p (r o)", r=PACK))
+        kw_win = big.tile([P, T], U32, name="kw_win", offset=0, align_bytes=64)
         nc.sync.dma_start(kw_win[:].bitcast(I32), k_words[0].rearrange("p t b -> p (t b)").bitcast(I32))
-
-        q_raw0 = load_q(0)
         for quad in range(4):
-            nc.scalar.dma_start(
+            nc.sync.dma_start(
                 ks_win[32 * quad : 32 * quad + 8, :].bitcast(I32),
                 k_scales[:, 4 * quad : 4 * quad + 4, :].bitcast(I32),
             )
-        nc.scalar.dma_start(nb_win[0:1, :], nb[0:1, :])
+        q_raw0 = load_q(0)
+        nc.sync.dma_start(nb_win[0:1, :], nb[0:1, :])
+        us_col = keep.tile([P, PACK], F32, name="us_col")
+        nc.vector.tensor_copy(us_col[:], us_stage[:, 0:PACK])
+        q_raw1 = load_q(1)
 
         warm = keep.tile([P, 1], F32, name="warm")
-        nc.scalar.activation(warm[:], us_col[:, 0:1], SILU)
+        nc.scalar.activation(warm[:], warm_in[:], SILU)
 
-        q_codes = keep.tile([P, 2, NQ], U32, name="q_codes", align_bytes=64)
+        q_codes = keep.tile([P, 2, NQ], U32, name="q_codes", tag="nb_win", align_bytes=64)
         q_scales = keep.tile([P, 2, NQ], U8, name="q_scales", align_bytes=64)
 
         def weave(copy, dst, src, c0, c1):
@@ -79,29 +84,37 @@ def tile_attend_mlpb_silu_kernel(tc, qT, k_words, k_scales, vT, nb, us, offs, ou
                 in_=grouped[:].rearrange("p w j -> p (w j)"),
             )
 
+        v_win = []
+
+        def load_v(c):
+            win = big.tile([P, T], F32, name=f"v_win{c}", offset=(3 + c) * SLOT, align_bytes=64)
+            nc.sync.dma_start(win[:], vT[P * c : P * (c + 1), :])
+            v_win.append(win)
+
+        load_v(0)
         kw_got = keep.tile([P, N], U32, name="kw_got", align_bytes=64)
         nc.vector.tensor_copy(kw_got[:], kw_win[:].indirect(offsets[:]))
-        q_raw1 = load_q(1)
-        ks_got = big.tile([P, N], U8, name="ks_got", tag="slot_b", align_bytes=64)
-        nc.vector.tensor_copy(ks_got[:], ks_win[:].indirect(offsets[:]))
+        ks_got = big.tile([P, 3 * SLOT], U8, name="ks_got", offset=4 * SLOT, align_bytes=64)
+        nc.vector.tensor_copy(ks_got[:, 0:N], ks_win[:].indirect(offsets[:]))
+        kw_dealt = keep.tile([P, 2, N], U16, name="kw_dealt", tag="ks_win", align_bytes=64)
+        kw_half = kw_got[:].bitcast(U16).rearrange("p (s r o) -> p o s r", r=PACK, o=2)
+        nc.vector.tensor_copy(kw_dealt[:, 0, :].rearrange("p (r s) -> p s r", r=PACK), kw_half[:, 0, :, :])
         ks_dealt = keep.tile([P, N], U8, name="ks_dealt", align_bytes=64)
         nc.vector.tensor_copy(
             ks_dealt[:].rearrange("p (r s) -> p s r", r=PACK),
-            ks_got[:].rearrange("p (s r) -> p s r", r=PACK),
+            ks_got[:, 0:N].rearrange("p (s r) -> p s r", r=PACK),
         )
         nc.sync.dma_start(ks_plane1[0:112, :].bitcast(I32), ks_dealt[4:116, :].bitcast(I32))
         ks_planes = [ks_dealt, ks_plane1]
-        kw_dealt = keep.tile([P, 2, N], U16, name="kw_dealt", align_bytes=64)
-        kw_half = kw_got[:].bitcast(U16).rearrange("p (s r o) -> p o s r", r=PACK, o=2)
-        for o in range(2):
-            nc.vector.tensor_copy(kw_dealt[:, o, :].rearrange("p (r s) -> p s r", r=PACK), kw_half[:, o, :, :])
-
-        q_grp0 = big.tile([P, NQ, PACK], BF16, name="q_grp0", tag="slot_d", align_bytes=64)
-        weave(nc.scalar.copy, q_grp0, q_raw0, 0, NQ)
-        quant(q_codes[:, 0, :], q_scales[:, 0, :], q_grp0, 0, NQ)
+        for c in range(1, 4):
+            load_v(c)
+        nc.vector.tensor_copy(kw_dealt[:, 1, :].rearrange("p (r s) -> p s r", r=PACK), kw_half[:, 1, :, :])
 
         nb_got = keep.tile([P, N], F32, name="nb_got", align_bytes=64)
         nc.vector.tensor_copy(nb_got[:], nb_win[:].indirect(offsets[:]))
+        q_grp0 = keep.tile([P, NQ, PACK], BF16, name="q_grp0", align_bytes=64)
+        weave(nc.scalar.copy, q_grp0, q_raw0, 0, NQ)
+        quant(q_codes[:, 0, :], q_scales[:, 0, :], q_grp0, 0, NQ)
 
         banks = [psum.tile([P, NQ], F32, name=f"a{r}", tag=f"bank{r}") for r in range(PACK)]
 
@@ -117,15 +130,6 @@ def tile_attend_mlpb_silu_kernel(tc, qT, k_words, k_scales, vT, nb, us, offs, ou
                 stop=(o == 1),
             )
 
-        for r in range(PACK):
-            first_layer(0, r)
-
-        v_win = []
-        for c in range(4):
-            win = big.tile([P, T], F32, name="v_win", tag="slot_" + "bcda"[c], align_bytes=64)
-            nc.sync.dma_start(win[:], vT[P * c : P * (c + 1), :])
-            v_win.append(win)
-
         q_grp1 = [keep.tile([P, 256, PACK], BF16, name=f"q_grp1_{h}", tag=f"q_grp1_{h}", align_bytes=64) for h in range(2)]
         weave(nc.vector.tensor_copy, q_grp1[0], q_raw1, 0, 256)
         weave(nc.scalar.copy, q_grp1[1], q_raw1, 256, NQ)
@@ -133,55 +137,79 @@ def tile_attend_mlpb_silu_kernel(tc, qT, k_words, k_scales, vT, nb, us, offs, ou
         nb_by_place = nb_got[:].rearrange("p (s r) -> p r s", r=PACK)
         for r in range(PACK):
             nc.tensor.transpose(nb_ps[:, r, :], nb_by_place[:, r, :], ident[:])
-        bias = keep.tile([P, PACK], F32, name="bias")
+        bias = big.tile([P, PACK], F32, name="bias", offset=2 * SLOT, align_bytes=64)
         nc.scalar.copy(bias[:], nb_ps[:, :, 0])
+
 
         quant(q_codes[:, 1, :], q_scales[:, 1, :], q_grp1[0], 0, 256)
         quant(q_codes[:, 1, :], q_scales[:, 1, :], q_grp1[1], 256, NQ)
         for r in range(PACK):
+            first_layer(0, r)
             first_layer(1, r)
 
-        v_codes = keep.tile([P, DV], U32, name="v_codes", align_bytes=64)
-        v_scales = keep.tile([P, DV], U8, name="v_scales", align_bytes=64)
+        v_codes = [
+            big.tile([P, 2 * P], U32, name="v_codes01", offset=5 * SLOT + 4096, align_bytes=64),
+            big.tile([P, P], U32, name="v_codes2", offset=6 * SLOT + 4096, align_bytes=64),
+            keep.tile([P, P], U32, name="v_codes3", align_bytes=64),
+        ]
+        v_scales = [keep.tile([P, w], U8, name=f"v_scales{i}", align_bytes=64) for i, w in enumerate((2 * P, P, P))]
 
         def gather_v(c, tag):
             got = keep.tile([P, N], BF16, name="v_got", tag=tag, align_bytes=64)
             nc.vector.tensor_copy(got[:], v_win[c][:].indirect(offsets[:]))
+            return got
+
+        def turn_v(c, got):
             words = got[:].bitcast(F32).rearrange("p (s u) -> p u s", u=2)
-            turned = psum.tile([P, 2, P], F32, name="turned", tag=f"bank{5 + c % 2}")
+            turned = psum.tile([P, 2, P], F32, name="turned", tag=f"bank{(0, 1, 4, 5)[c]}")
             for u in range(2):
                 nc.tensor.transpose(turned[:, u, :], words[:, u, :], ident[:])
-            grp = ring.tile([P, P, PACK], BF16, name="v_grp", align_bytes=64)
+            return turned
+
+        def drain_v(turned, grp):
             nc.scalar.copy(
-                grp[:].rearrange("p e j -> p (e j)").bitcast(F32).rearrange("p (e u) -> p e u", u=2),
+                grp.rearrange("p e j -> p (e j)").bitcast(F32).rearrange("p (e u) -> p e u", u=2),
                 turned[:].rearrange("p u e -> p e u"),
             )
-            return grp
-
-        def quant_v(c, grp):
-            quant(v_codes[:], v_scales[:], grp, P * c, P * (c + 1))
 
         act = [keep.tile([P, NQ], F32, name=f"act{r}", tag=f"act{r}", align_bytes=64) for r in range(PACK)]
-        y_rows = keep.tile([P, PACK, NQ], BF16, name="y_rows", align_bytes=64)
-        grp0 = gather_v(0, "q_grp1_1")
+        y_rows = big.tile([P, PACK, NQ], BF16, name="y_rows", offset=4 * SLOT, align_bytes=64)
+        got0 = gather_v(0, "q_grp1_1")
+        got1 = gather_v(1, "v_got1")
         for r in range(PACK):
             nc.scalar.activation(act[r][:], banks[r][:], SILU, bias=bias[:, r : r + 1])
-            nc.vector.tensor_scalar(y_rows[:, r, :], act[r][:], us_col[:, r : r + 1], None, MULT)
-        quant_v(0, grp0)
-        grp1 = gather_v(1, "act1")
+            if r < 3:
+                nc.vector.tensor_scalar(y_rows[:, r, :], act[r][:], us_col[:, r : r + 1], None, MULT)
+            else:
+                nc.scalar.activation(y_rows[:, r, :], act[r][:], COPY, scale=us_col[:, r : r + 1])
+        turned0 = turn_v(0, got0)
+        turned1 = turn_v(1, got1)
+        turned2 = turn_v(2, gather_v(2, "act2"))
 
-        y_grp = [keep.tile([P, 256, PACK], BF16, name=f"y_grp{h}", tag=f"y_grp{h}", align_bytes=64) for h in range(2)]
+        y_grp = [
+            big.tile([P, 256, PACK], BF16, name="y_grp0", offset=5 * SLOT, align_bytes=64),
+            keep.tile([P, 256, PACK], BF16, name="y_grp1", tag="y_grp1", align_bytes=64),
+        ]
         y_codes = keep.tile([P, NQ], U32, name="y_codes", align_bytes=64)
         y_scales = keep.tile([P, NQ], U8, name="y_scales", align_bytes=64)
         weave(nc.vector.tensor_copy, y_grp[0], y_rows, 0, 256)
         weave(nc.scalar.copy, y_grp[1], y_rows, 256, NQ)
-        quant_v(1, grp1)
+        v_grp01 = keep.tile([P, 2 * P, PACK], BF16, name="v_grp01", align_bytes=64)
+        drain_v(turned0, v_grp01[:, 0:P, :])
+        drain_v(turned1, v_grp01[:, P : 2 * P, :])
+        quant(v_codes[0][:], v_scales[0][:], v_grp01, 0, 2 * P)
         quant(y_codes[:], y_scales[:], y_grp[0], 0, 256)
         quant(y_codes[:], y_scales[:], y_grp[1], 256, NQ)
+        v_grp2 = keep.tile([P, P, PACK], BF16, name="v_grp2", align_bytes=64)
+        drain_v(turned2, v_grp2[:])
+        turned3 = turn_v(3, gather_v(3, "y_grp1"))
+        quant(v_codes[1][:], v_scales[1][:], v_grp2, 0, P)
+        v_grp3 = keep.tile([P, P, PACK], BF16, name="v_grp3", align_bytes=64)
+        drain_v(turned3, v_grp3[:])
 
         out_rows = out[0].rearrange("(j p) e -> p j e", p=P)
 
-        def second_layer(e0, width, j0, nj, tag, copy):
+        def second_layer(part, e0, width, j0, nj, tag, copy, res):
             acc = psum.tile([P, nj, width], F32, name="acc", tag=tag)
             for j in range(nj):
                 rows = slice(P * (j0 + j), P * (j0 + j + 1))
@@ -189,21 +217,22 @@ def tile_attend_mlpb_silu_kernel(tc, qT, k_words, k_scales, vT, nb, us, offs, ou
                     out=acc[:, j, :],
                     lhsT=y_codes[:, rows].bitcast(FP8X4),
                     lhsT_scale=y_scales[:, rows],
-                    rhs=v_codes[:, e0 : e0 + width].bitcast(FP8X4),
-                    rhs_scale=v_scales[:, e0 : e0 + width],
+                    rhs=v_codes[part][:].bitcast(FP8X4),
+                    rhs_scale=v_scales[part][:],
                     start=True,
                     stop=True,
                 )
-            res = keep.tile([P, nj, width], F32, name=f"res_{e0}_{j0}")
             copy(res[:], acc[:])
             nc.sync.dma_start(out_rows[:, j0 : j0 + nj, e0 : e0 + width], res[:])
 
-        grp2 = gather_v(2, "y_grp0")
-        second_layer(0, 256, 0, 2, "bank0", nc.scalar.copy)
-        second_layer(0, 256, 2, 2, "bank1", nc.scalar.copy)
-        quant_v(2, grp2)
-        second_layer(256, 128, 0, 4, "bank2", nc.scalar.copy)
-        grp3 = gather_v(3, "y_grp1")
-        quant_v(3, grp3)
-        second_layer(384, 128, 0, 2, "bank3", nc.scalar.copy)
-        second_layer(384, 128, 2, 2, "bank7", nc.vector.tensor_copy)
+        res_a = keep.tile([P, 2, 256], F32, name="res_a")
+        second_layer(0, 0, 256, 0, 2, "bank2", nc.scalar.copy, res_a)
+        res_b = big.tile([P, 2, 256], F32, name="res_b", offset=6 * SLOT, align_bytes=64)
+        second_layer(0, 0, 256, 2, 2, "bank3", nc.vector.tensor_copy, res_b)
+        quant(v_codes[2][:], v_scales[2][:], v_grp3, 0, P)
+        res_c = keep.tile([P, 4, 128], F32, name="res_c")
+        second_layer(1, 256, 128, 0, 4, "bank6", nc.scalar.copy, res_c)
+        res_d = keep.tile([P, 2, 128], F32, name="res_d")
+        res_e = keep.tile([P, 2, 128], F32, name="res_e")
+        second_layer(2, 384, 128, 0, 2, "bank0", nc.scalar.copy, res_d)
+        second_layer(2, 384, 128, 2, 2, "bank7", nc.vector.tensor_copy, res_e)

@@ -16,7 +16,7 @@ U8 = mybir.dt.uint8
 FP8X4 = mybir.dt.float8_e4m3fn_x4
 FP4X4 = mybir.dt.float4_e2m1fn_x4
 SILU = mybir.ActivationFunctionType.Silu
-COPY = mybir.ActivationFunctionType.Copy
+ADD = mybir.AluOpType.add
 MULT = mybir.AluOpType.mult
 
 P = 128
@@ -34,41 +34,41 @@ def tile_attend_mlpb_silu_kernel(tc, qT, k_words, k_scales, vT, nb, us, offs, ou
         offsets = keep.tile([P, N // 16], U16, name="offsets")
         nc.sync.dma_start(offsets[:], offs)
 
-        ks_win = keep.tile([P, T], U8, name="ks_win", tag="ks_win", align_bytes=64)
+        ks_win = keep.tile([P, T], U8, name="ks_win", align_bytes=64)
         nb_win = keep.tile([P, T], F32, name="nb_win", tag="nb_win", align_bytes=64)
         ks_plane1 = keep.tile([P, N], U8, name="ks_plane1", align_bytes=64)
-        nc.vector.memset(ks_win[:].bitcast(I32), 0)
+        nc.gpsimd.memset(ks_win[:].bitcast(I32), 0)
         nc.vector.memset(nb_win[:], 0.0)
-        warm_in = keep.tile([P, 1], F32, name="warm_in")
-        nc.vector.memset(warm_in[:], 0.0)
-        nc.vector.memset(ks_plane1[:].bitcast(I32), 0)
         ident = keep.tile([P, P], F32, name="ident")
         make_identity(nc, ident[:])
 
         def load_q(o):
-            raw = big.tile([P, PACK, NQ], F32, name=f"q_raw{o}", offset=(1 + o) * SLOT, align_bytes=64)
+            raw = big.tile([P, PACK, NQ], F32, name=f"q_raw{o}", offset=2 * o * SLOT, align_bytes=64)
             nc.sync.dma_start(raw[:], qT[0, 512 * o : 512 * (o + 1), :].rearrange("(p j) w -> p j w", j=PACK))
             return raw
 
-        us_stage = big.tile([P, 2 * T], F32, name="us_stage", offset=2 * SLOT, align_bytes=64)
+        us_stage = big.tile([P, 3 * T], F32, name="us_stage", offset=SLOT, align_bytes=64)
         nc.sync.dma_start(us_stage[:, 0:PACK], us[0].rearrange("(p r) o -> p (r o)", r=PACK))
-        kw_win = big.tile([P, T], U32, name="kw_win", offset=0, align_bytes=64)
-        nc.sync.dma_start(kw_win[:].bitcast(I32), k_words[0].rearrange("p t b -> p (t b)").bitcast(I32))
+        q_raw0 = load_q(0)
         for quad in range(4):
             nc.sync.dma_start(
                 ks_win[32 * quad : 32 * quad + 8, :].bitcast(I32),
                 k_scales[:, 4 * quad : 4 * quad + 4, :].bitcast(I32),
             )
-        q_raw0 = load_q(0)
         nc.sync.dma_start(nb_win[0:1, :], nb[0:1, :])
         us_col = keep.tile([P, PACK], F32, name="us_col")
         nc.vector.tensor_copy(us_col[:], us_stage[:, 0:PACK])
+        kw_win = big.tile([P, T], U32, name="kw_win", offset=SLOT, align_bytes=64)
+        nc.sync.dma_start(kw_win[:].bitcast(I32), k_words[0].rearrange("p t b -> p (t b)").bitcast(I32))
         q_raw1 = load_q(1)
 
+        warm_in = keep.tile([P, 1], F32, name="warm_in")
+        nc.vector.memset(warm_in[:], 0.0)
+        nc.vector.memset(ks_plane1[:].bitcast(I32), 0)
         warm = keep.tile([P, 1], F32, name="warm")
         nc.scalar.activation(warm[:], warm_in[:], SILU)
 
-        q_codes = keep.tile([P, 2, NQ], U32, name="q_codes", tag="nb_win", align_bytes=64)
+        q_codes = big.tile([P, 2, NQ], U32, name="q_codes", offset=SLOT, align_bytes=64)
         q_scales = keep.tile([P, 2, NQ], U8, name="q_scales", align_bytes=64)
 
         def weave(copy, dst, src, c0, c1):
@@ -92,14 +92,11 @@ def tile_attend_mlpb_silu_kernel(tc, qT, k_words, k_scales, vT, nb, us, offs, ou
             v_win.append(win)
 
         load_v(0)
-        kw_got = keep.tile([P, N], U32, name="kw_got", align_bytes=64)
-        nc.vector.tensor_copy(kw_got[:], kw_win[:].indirect(offsets[:]))
         ks_got = big.tile([P, 3 * SLOT], U8, name="ks_got", offset=4 * SLOT, align_bytes=64)
         nc.vector.tensor_copy(ks_got[:, 0:N], ks_win[:].indirect(offsets[:]))
-        kw_dealt = keep.tile([P, 2, N], U16, name="kw_dealt", tag="ks_win", align_bytes=64)
-        kw_half = kw_got[:].bitcast(U16).rearrange("p (s r o) -> p o s r", r=PACK, o=2)
-        nc.vector.tensor_copy(kw_dealt[:, 0, :].rearrange("p (r s) -> p s r", r=PACK), kw_half[:, 0, :, :])
-        ks_dealt = keep.tile([P, N], U8, name="ks_dealt", align_bytes=64)
+        nb_got = keep.tile([P, N], F32, name="nb_got", align_bytes=64)
+        nc.vector.tensor_copy(nb_got[:], nb_win[:].indirect(offsets[:]))
+        ks_dealt = keep.tile([P, N], U8, name="ks_dealt", tag="nb_win", align_bytes=64)
         nc.vector.tensor_copy(
             ks_dealt[:].rearrange("p (r s) -> p s r", r=PACK),
             ks_got[:, 0:N].rearrange("p (s r) -> p s r", r=PACK),
@@ -108,13 +105,16 @@ def tile_attend_mlpb_silu_kernel(tc, qT, k_words, k_scales, vT, nb, us, offs, ou
         ks_planes = [ks_dealt, ks_plane1]
         for c in range(1, 4):
             load_v(c)
-        nc.vector.tensor_copy(kw_dealt[:, 1, :].rearrange("p (r s) -> p s r", r=PACK), kw_half[:, 1, :, :])
 
-        nb_got = keep.tile([P, N], F32, name="nb_got", align_bytes=64)
-        nc.vector.tensor_copy(nb_got[:], nb_win[:].indirect(offsets[:]))
+        kw_got = keep.tile([P, N], U32, name="kw_got", align_bytes=64)
+        nc.vector.tensor_copy(kw_got[:], kw_win[:].indirect(offsets[:]))
         q_grp0 = keep.tile([P, NQ, PACK], BF16, name="q_grp0", align_bytes=64)
         weave(nc.scalar.copy, q_grp0, q_raw0, 0, NQ)
         quant(q_codes[:, 0, :], q_scales[:, 0, :], q_grp0, 0, NQ)
+        kw_dealt = [keep.tile([P, N], U16, name=f"kw_dealt{o}", align_bytes=64) for o in range(2)]
+        kw_half = kw_got[:].bitcast(U16).rearrange("p (s r o) -> p o s r", r=PACK, o=2)
+        for o in range(2):
+            nc.vector.tensor_copy(kw_dealt[o][:].rearrange("p (r s) -> p s r", r=PACK), kw_half[:, o, :, :])
 
         banks = [psum.tile([P, NQ], F32, name=f"a{r}", tag=f"bank{r}") for r in range(PACK)]
 
@@ -122,7 +122,7 @@ def tile_attend_mlpb_silu_kernel(tc, qT, k_words, k_scales, vT, nb, us, offs, ou
             cols = slice(P * r, P * (r + 1))
             nc.tensor.matmul_mx(
                 out=banks[r][:],
-                lhsT=kw_dealt[:, o, cols].bitcast(FP4X4),
+                lhsT=kw_dealt[o][:, cols].bitcast(FP4X4),
                 lhsT_scale=ks_planes[o][:, cols],
                 rhs=q_codes[:, o, :].bitcast(FP8X4),
                 rhs_scale=q_scales[:, o, :],
@@ -149,19 +149,18 @@ def tile_attend_mlpb_silu_kernel(tc, qT, k_words, k_scales, vT, nb, us, offs, ou
 
         v_codes = [
             big.tile([P, 2 * P], U32, name="v_codes01", offset=5 * SLOT + 4096, align_bytes=64),
-            big.tile([P, P], U32, name="v_codes2", offset=6 * SLOT + 4096, align_bytes=64),
+            keep.tile([P, P], U32, name="v_codes2", align_bytes=64),
             keep.tile([P, P], U32, name="v_codes3", align_bytes=64),
         ]
         v_scales = [keep.tile([P, w], U8, name=f"v_scales{i}", align_bytes=64) for i, w in enumerate((2 * P, P, P))]
 
-        def gather_v(c, tag):
-            got = keep.tile([P, N], BF16, name="v_got", tag=tag, align_bytes=64)
-            nc.vector.tensor_copy(got[:], v_win[c][:].indirect(offsets[:]))
+        def gather_v(c, got):
+            nc.vector.tensor_copy(got, v_win[c][:].indirect(offsets[:]))
             return got
 
         def turn_v(c, got):
-            words = got[:].bitcast(F32).rearrange("p (s u) -> p u s", u=2)
-            turned = psum.tile([P, 2, P], F32, name="turned", tag=f"bank{(0, 1, 4, 5)[c]}")
+            words = got.bitcast(F32).rearrange("p (s u) -> p u s", u=2)
+            turned = psum.tile([P, 2, P], F32, name="turned", tag=f"bank{(0, 1, 4, 2)[c]}")
             for u in range(2):
                 nc.tensor.transpose(turned[:, u, :], words[:, u, :], ident[:])
             return turned
@@ -173,39 +172,34 @@ def tile_attend_mlpb_silu_kernel(tc, qT, k_words, k_scales, vT, nb, us, offs, ou
             )
 
         act = [keep.tile([P, NQ], F32, name=f"act{r}", tag=f"act{r}", align_bytes=64) for r in range(PACK)]
-        y_rows = big.tile([P, PACK, NQ], BF16, name="y_rows", offset=4 * SLOT, align_bytes=64)
-        got0 = gather_v(0, "q_grp1_1")
-        got1 = gather_v(1, "v_got1")
+        y_rows = keep.tile([P, PACK, NQ], BF16, name="y_rows", align_bytes=64)
+        got0 = gather_v(0, keep.tile([P, N], BF16, name="v_got0", tag="q_grp1_1", align_bytes=64)[:])
+        got1 = gather_v(1, keep.tile([P, N], BF16, name="v_got1", tag="v_got1", align_bytes=64)[:])
         for r in range(PACK):
             nc.scalar.activation(act[r][:], banks[r][:], SILU, bias=bias[:, r : r + 1])
-            if r < 3:
-                nc.vector.tensor_scalar(y_rows[:, r, :], act[r][:], us_col[:, r : r + 1], None, MULT)
-            else:
-                nc.scalar.activation(y_rows[:, r, :], act[r][:], COPY, scale=us_col[:, r : r + 1])
+            nc.gpsimd.tensor_scalar(y_rows[:, r, :], act[r][:], us_col[:, r : r + 1], 0.0, MULT, ADD)
         turned0 = turn_v(0, got0)
         turned1 = turn_v(1, got1)
-        turned2 = turn_v(2, gather_v(2, "act2"))
+        turned2 = turn_v(2, gather_v(2, keep.tile([P, N], BF16, name="v_got2", tag="v_got2", align_bytes=64)[:]))
 
         y_grp = [
             big.tile([P, 256, PACK], BF16, name="y_grp0", offset=5 * SLOT, align_bytes=64),
-            keep.tile([P, 256, PACK], BF16, name="y_grp1", tag="y_grp1", align_bytes=64),
+            big.tile([P, 256, PACK], BF16, name="y_grp1", offset=2048, align_bytes=64),
         ]
-        y_codes = keep.tile([P, NQ], U32, name="y_codes", align_bytes=64)
+        y_codes = big.tile([P, NQ], U32, name="y_codes", offset=5 * SLOT + 2048, align_bytes=64)
         y_scales = keep.tile([P, NQ], U8, name="y_scales", align_bytes=64)
         weave(nc.vector.tensor_copy, y_grp[0], y_rows, 0, 256)
         weave(nc.scalar.copy, y_grp[1], y_rows, 256, NQ)
-        v_grp01 = keep.tile([P, 2 * P, PACK], BF16, name="v_grp01", align_bytes=64)
+        v_grp01 = big.tile([P, 2 * P, PACK], BF16, name="v_grp01", offset=0, align_bytes=64)
         drain_v(turned0, v_grp01[:, 0:P, :])
         drain_v(turned1, v_grp01[:, P : 2 * P, :])
         quant(v_codes[0][:], v_scales[0][:], v_grp01, 0, 2 * P)
         quant(y_codes[:], y_scales[:], y_grp[0], 0, 256)
         quant(y_codes[:], y_scales[:], y_grp[1], 256, NQ)
-        v_grp2 = keep.tile([P, P, PACK], BF16, name="v_grp2", align_bytes=64)
+        v_grp2 = big.tile([P, P, PACK], BF16, name="v_grp2", offset=4096, align_bytes=64)
         drain_v(turned2, v_grp2[:])
-        turned3 = turn_v(3, gather_v(3, "y_grp1"))
         quant(v_codes[1][:], v_scales[1][:], v_grp2, 0, P)
-        v_grp3 = keep.tile([P, P, PACK], BF16, name="v_grp3", align_bytes=64)
-        drain_v(turned3, v_grp3[:])
+        got3 = gather_v(3, big.tile([P, 5 * N], BF16, name="v_got3", offset=0, align_bytes=64)[:, 0:N])
 
         out_rows = out[0].rearrange("(j p) e -> p j e", p=P)
 
@@ -229,9 +223,12 @@ def tile_attend_mlpb_silu_kernel(tc, qT, k_words, k_scales, vT, nb, us, offs, ou
         second_layer(0, 0, 256, 0, 2, "bank2", nc.scalar.copy, res_a)
         res_b = big.tile([P, 2, 256], F32, name="res_b", offset=6 * SLOT, align_bytes=64)
         second_layer(0, 0, 256, 2, 2, "bank3", nc.vector.tensor_copy, res_b)
+        res_c = big.tile([P, 4, 128], F32, name="res_c", offset=6 * SLOT + 2048, align_bytes=64)
+        second_layer(1, 256, 128, 0, 4, "bank6", nc.vector.tensor_copy, res_c)
+        turned3 = turn_v(3, got3)
+        v_grp3 = keep.tile([P, P, PACK], BF16, name="v_grp3", align_bytes=64)
+        drain_v(turned3, v_grp3[:])
         quant(v_codes[2][:], v_scales[2][:], v_grp3, 0, P)
-        res_c = keep.tile([P, 4, 128], F32, name="res_c")
-        second_layer(1, 256, 128, 0, 4, "bank6", nc.scalar.copy, res_c)
         res_d = keep.tile([P, 2, 128], F32, name="res_d")
         res_e = keep.tile([P, 2, 128], F32, name="res_e")
         second_layer(2, 384, 128, 0, 2, "bank0", nc.scalar.copy, res_d)

@@ -16,6 +16,7 @@ U8 = mybir.dt.uint8
 FP8X4 = mybir.dt.float8_e4m3fn_x4
 FP4X4 = mybir.dt.float4_e2m1fn_x4
 SILU = mybir.ActivationFunctionType.Silu
+COPY = mybir.ActivationFunctionType.Copy
 ADD = mybir.AluOpType.add
 MULT = mybir.AluOpType.mult
 
@@ -165,8 +166,8 @@ def tile_attend_mlpb_silu_kernel(tc, qT, k_words, k_scales, vT, nb, us, offs, ou
                 nc.tensor.transpose(turned[:, u, :], words[:, u, :], ident[:])
             return turned
 
-        def drain_v(turned, grp):
-            nc.scalar.copy(
+        def drain_v(copy, turned, grp):
+            copy(
                 grp.rearrange("p e j -> p (e j)").bitcast(F32).rearrange("p (e u) -> p e u", u=2),
                 turned[:].rearrange("p u e -> p e u"),
             )
@@ -177,29 +178,32 @@ def tile_attend_mlpb_silu_kernel(tc, qT, k_words, k_scales, vT, nb, us, offs, ou
         got1 = gather_v(1, keep.tile([P, N], BF16, name="v_got1", tag="v_got1", align_bytes=64)[:])
         for r in range(PACK):
             nc.scalar.activation(act[r][:], banks[r][:], SILU, bias=bias[:, r : r + 1])
-            nc.gpsimd.tensor_scalar(y_rows[:, r, :], act[r][:], us_col[:, r : r + 1], 0.0, MULT, ADD)
+            if r < 3:
+                nc.gpsimd.tensor_scalar(y_rows[:, r, :], act[r][:], us_col[:, r : r + 1], 0.0, MULT, ADD)
+            else:
+                nc.scalar.activation(y_rows[:, r, :], act[r][:], COPY, scale=us_col[:, r : r + 1])
         turned0 = turn_v(0, got0)
         turned1 = turn_v(1, got1)
+        v_grp01 = big.tile([P, 2 * P, PACK], BF16, name="v_grp01", offset=4 * SLOT, align_bytes=64)
+        drain_v(nc.vector.tensor_copy, turned0, v_grp01[:, 0:P, :])
+        drain_v(nc.vector.tensor_copy, turned1, v_grp01[:, P : 2 * P, :])
         turned2 = turn_v(2, gather_v(2, keep.tile([P, N], BF16, name="v_got2", tag="v_got2", align_bytes=64)[:]))
 
         y_grp = [
             big.tile([P, 256, PACK], BF16, name="y_grp0", offset=5 * SLOT, align_bytes=64),
-            big.tile([P, 256, PACK], BF16, name="y_grp1", offset=2048, align_bytes=64),
+            big.tile([P, 256, PACK], BF16, name="y_grp1", offset=4 * SLOT + 2048, align_bytes=64),
         ]
         y_codes = big.tile([P, NQ], U32, name="y_codes", offset=5 * SLOT + 2048, align_bytes=64)
         y_scales = keep.tile([P, NQ], U8, name="y_scales", align_bytes=64)
         weave(nc.vector.tensor_copy, y_grp[0], y_rows, 0, 256)
         weave(nc.scalar.copy, y_grp[1], y_rows, 256, NQ)
-        v_grp01 = big.tile([P, 2 * P, PACK], BF16, name="v_grp01", offset=0, align_bytes=64)
-        drain_v(turned0, v_grp01[:, 0:P, :])
-        drain_v(turned1, v_grp01[:, P : 2 * P, :])
         quant(v_codes[0][:], v_scales[0][:], v_grp01, 0, 2 * P)
         quant(y_codes[:], y_scales[:], y_grp[0], 0, 256)
         quant(y_codes[:], y_scales[:], y_grp[1], 256, NQ)
-        v_grp2 = big.tile([P, P, PACK], BF16, name="v_grp2", offset=4096, align_bytes=64)
-        drain_v(turned2, v_grp2[:])
+        v_grp2 = keep.tile([P, P, PACK], BF16, name="v_grp2", align_bytes=64)
+        drain_v(nc.scalar.copy, turned2, v_grp2[:])
         quant(v_codes[1][:], v_scales[1][:], v_grp2, 0, P)
-        got3 = gather_v(3, big.tile([P, 5 * N], BF16, name="v_got3", offset=0, align_bytes=64)[:, 0:N])
+        got3 = gather_v(3, big.tile([P, 4 * N], BF16, name="v_got3", offset=4 * SLOT, align_bytes=64)[:, 0:N])
 
         out_rows = out[0].rearrange("(j p) e -> p j e", p=P)
 
@@ -227,7 +231,7 @@ def tile_attend_mlpb_silu_kernel(tc, qT, k_words, k_scales, vT, nb, us, offs, ou
         second_layer(1, 256, 128, 0, 4, "bank6", nc.vector.tensor_copy, res_c)
         turned3 = turn_v(3, got3)
         v_grp3 = keep.tile([P, P, PACK], BF16, name="v_grp3", align_bytes=64)
-        drain_v(turned3, v_grp3[:])
+        drain_v(nc.scalar.copy, turned3, v_grp3[:])
         quant(v_codes[2][:], v_scales[2][:], v_grp3, 0, P)
         res_d = keep.tile([P, 2, 128], F32, name="res_d")
         res_e = keep.tile([P, 2, 128], F32, name="res_e")

from contextlib import ExitStack

import concourse.mybir as mybir
from concourse.masks import make_identity

N, T, D, NQ, DV = 512, 2048, 1024, 512, 512
FLOPS = 2 * N * NQ * D + 2 * N * NQ * DV
BYTES = 4 * D * NQ + 128 * T * 4 + 32 * T + 4 * DV * T + 4 * T + 4 * N + 128 * (N // 16) * 2 + 4 * NQ * DV

F32 = mybir.dt.float32
BF16 = mybir.dt.bfloat16
I32 = mybir.dt.int32
U32 = mybir.dt.uint32
U16 = mybir.dt.uint16
U8 = mybir.dt.uint8
FP8X4 = mybir.dt.float8_e4m3fn_x4
FP4X4 = mybir.dt.float4_e2m1fn_x4
SILU = mybir.ActivationFunctionType.Silu
COPY = mybir.ActivationFunctionType.Copy
ADD = mybir.AluOpType.add
MULT = mybir.AluOpType.mult

P = 128
PACK = 4
SLOT = 4 * T


def tile_attend_mlpb_silu_kernel(tc, qT, k_words, k_scales, vT, nb, us, offs, out):
    nc = tc.nc
    with ExitStack() as ctx:
        keep = ctx.enter_context(tc.tile_pool(name="keep", bufs=1))
        big = ctx.enter_context(tc.tile_pool(name="big", bufs=1))
        psum = ctx.enter_context(tc.psum_pool(name="psum", bufs=1))

        offsets = keep.tile([P, N // 16], U16, name="offsets")
        nc.sync.dma_start(offsets[:], offs)

        ks_win = keep.tile([P, T], U8, name="ks_win", align_bytes=64)
        nb_win = keep.tile([P, T], F32, name="nb_win", tag="nb_win", align_bytes=64)
        ks_plane1 = keep.tile([P, N], U8, name="ks_plane1", align_bytes=64)
        nc.gpsimd.memset(ks_win[:].bitcast(I32), 0)
        nc.vector.memset(nb_win[:], 0.0)
        ident = keep.tile([P, P], F32, name="ident")
        make_identity(nc, ident[:])

        def load_q(o):
            raw = big.tile([P, PACK, NQ], F32, name=f"q_raw{o}", offset=2 * o * SLOT, align_bytes=64)
            nc.sync.dma_start(raw[:], qT[0, 512 * o : 512 * (o + 1), :].rearrange("(p j) w -> p j w", j=PACK))
            return raw

        us_stage = big.tile([P, 3 * T], F32, name="us_stage", offset=SLOT, align_bytes=64)
        nc.sync.dma_start(us_stage[:, 0:PACK], us[0].rearrange("(p r) o -> p (r o)", r=PACK))
        q_raw0 = load_q(0)
        for quad in range(4):
            nc.sync.dma_start(
                ks_win[32 * quad : 32 * quad + 8, :].bitcast(I32),
                k_scales[:, 4 * quad : 4 * quad + 4, :].bitcast(I32),
            )
        nc.sync.dma_start(nb_win[0:1, :], nb[0:1, :])
        us_col = keep.tile([P, PACK], F32, name="us_col")
        nc.vector.tensor_copy(us_col[:], us_stage[:, 0:PACK])
        kw_win = big.tile([P, T], U32, name="kw_win", offset=SLOT, align_bytes=64)
        nc.sync.dma_start(kw_win[:].bitcast(I32), k_words[0].rearrange("p t b -> p (t b)").bitcast(I32))
        q_raw1 = load_q(1)

        warm_in = keep.tile([P, 1], F32, name="warm_in")
        nc.vector.memset(warm_in[:], 0.0)
        nc.vector.memset(ks_plane1[:].bitcast(I32), 0)
        warm = keep.tile([P, 1], F32, name="warm")
        nc.scalar.activation(warm[:], warm_in[:], SILU)

        q_codes = big.tile([P, 2, NQ], U32, name="q_codes", offset=SLOT, align_bytes=64)
        q_scales = keep.tile([P, 2, NQ], U8, name="q_scales", align_bytes=64)

        def weave(copy, dst, src, c0, c1):
            copy(
                dst[:].rearrange("p (c i) t -> p c t i", i=4),
                src[:, :, c0:c1].rearrange("p t (c i) -> p c t i", i=4),
            )

        def quant(codes, scales, grouped, c0, c1):
            nc.vector.quantize_mx(
                out=codes[:, c0:c1].bitcast(FP8X4),
                scales=scales[:, c0:c1],
                in_=grouped[:].rearrange("p w j -> p (w j)"),
            )

        v_win = []

        def load_v(c):
            win = big.tile([P, T], F32, name=f"v_win{c}", offset=(3 + c) * SLOT, align_bytes=64)
            nc.sync.dma_start(win[:], vT[P * c : P * (c + 1), :])
            v_win.append(win)

        load_v(0)
        ks_got = big.tile([P, 3 * SLOT], U8, name="ks_got", offset=4 * SLOT, align_bytes=64)
        nc.vector.tensor_copy(ks_got[:, 0:N], ks_win[:].indirect(offsets[:]))
        nb_got = keep.tile([P, N], F32, name="nb_got", align_bytes=64)
        nc.vector.tensor_copy(nb_got[:], nb_win[:].indirect(offsets[:]))
        ks_dealt = keep.tile([P, N], U8, name="ks_dealt", tag="nb_win", align_bytes=64)
        nc.vector.tensor_copy(
            ks_dealt[:].rearrange("p (r s) -> p s r", r=PACK),
            ks_got[:, 0:N].rearrange("p (s r) -> p s r", r=PACK),
        )
        nc.sync.dma_start(ks_plane1[0:112, :].bitcast(I32), ks_dealt[4:116, :].bitcast(I32))
        ks_planes = [ks_dealt, ks_plane1]
        for c in range(1, 4):
            load_v(c)

        kw_got = keep.tile([P, N], U32, name="kw_got", align_bytes=64)
        nc.vector.tensor_copy(kw_got[:], kw_win[:].indirect(offsets[:]))
        q_grp0 = keep.tile([P, NQ, PACK], BF16, name="q_grp0", align_bytes=64)
        weave(nc.scalar.copy, q_grp0, q_raw0, 0, NQ)
        quant(q_codes[:, 0, :], q_scales[:, 0, :], q_grp0, 0, NQ)
        kw_dealt = [keep.tile([P, N], U16, name=f"kw_dealt{o}", align_bytes=64) for o in range(2)]
        kw_half = kw_got[:].bitcast(U16).rearrange("p (s r o) -> p o s r", r=PACK, o=2)
        for o in range(2):
            nc.vector.tensor_copy(kw_dealt[o][:].rearrange("p (r s) -> p s r", r=PACK), kw_half[:, o, :, :])

        banks = [psum.tile([P, NQ], F32, name=f"a{r}", tag=f"bank{r}") for r in range(PACK)]

        def first_layer(o, r):
            cols = slice(P * r, P * (r + 1))
            nc.tensor.matmul_mx(
                out=banks[r][:],
                lhsT=kw_dealt[o][:, cols].bitcast(FP4X4),
                lhsT_scale=ks_planes[o][:, cols],
                rhs=q_codes[:, o, :].bitcast(FP8X4),
                rhs_scale=q_scales[:, o, :],
                start=(o == 0),
                stop=(o == 1),
            )

        q_grp1 = [keep.tile([P, 256, PACK], BF16, name=f"q_grp1_{h}", tag=f"q_grp1_{h}", align_bytes=64) for h in range(2)]
        weave(nc.vector.tensor_copy, q_grp1[0], q_raw1, 0, 256)
        weave(nc.scalar.copy, q_grp1[1], q_raw1, 256, NQ)
        nb_ps = psum.tile([P, PACK, P], F32, name="nb_ps", tag="bank4")
        nb_by_place = nb_got[:].rearrange("p (s r) -> p r s", r=PACK)
        for r in range(PACK):
            nc.tensor.transpose(nb_ps[:, r, :], nb_by_place[:, r, :], ident[:])
        bias = big.tile([P, PACK], F32, name="bias", offset=2 * SLOT, align_bytes=64)
        nc.scalar.copy(bias[:], nb_ps[:, :, 0])


        quant(q_codes[:, 1, :], q_scales[:, 1, :], q_grp1[0], 0, 256)
        quant(q_codes[:, 1, :], q_scales[:, 1, :], q_grp1[1], 256, NQ)
        for r in range(PACK):
            first_layer(0, r)
            first_layer(1, r)

        v_codes = [
            big.tile([P, 2 * P], U32, name="v_codes01", offset=5 * SLOT + 4096, align_bytes=64),
            keep.tile([P, P], U32, name="v_codes2", align_bytes=64),
            keep.tile([P, P], U32, name="v_codes3", align_bytes=64),
        ]
        v_scales = [keep.tile([P, w], U8, name=f"v_scales{i}", align_bytes=64) for i, w in enumerate((2 * P, P, P))]

        def gather_v(c, got):
            nc.vector.tensor_copy(got, v_win[c][:].indirect(offsets[:]))
            return got

        def turn_v(c, got):
            words = got.bitcast(F32).rearrange("p (s u) -> p u s", u=2)
            turned = psum.tile([P, 2, P], F32, name="turned", tag=f"bank{(0, 1, 4, 2)[c]}")
            for u in range(2):
                nc.tensor.transpose(turned[:, u, :], words[:, u, :], ident[:])
            return turned

        def drain_v(copy, turned, grp):
            copy(
                grp.rearrange("p e j -> p (e j)").bitcast(F32).rearrange("p (e u) -> p e u", u=2),
                turned[:].rearrange("p u e -> p e u"),
            )

        act = [keep.tile([P, NQ], F32, name=f"act{r}", tag=f"act{r}", align_bytes=64) for r in range(PACK)]
        y_rows = keep.tile([P, PACK, NQ], BF16, name="y_rows", align_bytes=64)
        got0 = gather_v(0, keep.tile([P, N], BF16, name="v_got0", tag="q_grp1_1", align_bytes=64)[:])
        got1 = gather_v(1, keep.tile([P, N], BF16, name="v_got1", tag="v_got1", align_bytes=64)[:])
        for r in range(PACK):
            nc.scalar.activation(act[r][:], banks[r][:], SILU, bias=bias[:, r : r + 1])
            if r < 3:
                nc.gpsimd.tensor_scalar(y_rows[:, r, :], act[r][:], us_col[:, r : r + 1], 0.0, MULT, ADD)
            else:
                nc.scalar.activation(y_rows[:, r, :], act[r][:], COPY, scale=us_col[:, r : r + 1])
        turned0 = turn_v(0, got0)
        turned1 = turn_v(1, got1)
        v_grp01 = big.tile([P, 2 * P, PACK], BF16, name="v_grp01", offset=4 * SLOT, align_bytes=64)
        drain_v(nc.vector.tensor_copy, turned0, v_grp01[:, 0:P, :])
        drain_v(nc.vector.tensor_copy, turned1, v_grp01[:, P : 2 * P, :])
        turned2 = turn_v(2, gather_v(2, keep.tile([P, N], BF16, name="v_got2", tag="v_got2", align_bytes=64)[:]))

        y_grp = [
            big.tile([P, 256, PACK], BF16, name="y_grp0", offset=5 * SLOT, align_bytes=64),
            big.tile([P, 256, PACK], BF16, name="y_grp1", offset=4 * SLOT + 2048, align_bytes=64),
        ]
        y_codes = big.tile([P, NQ], U32, name="y_codes", offset=5 * SLOT + 2048, align_bytes=64)
        y_scales = keep.tile([P, NQ], U8, name="y_scales", align_bytes=64)
        weave(nc.vector.tensor_copy, y_grp[0], y_rows, 0, 256)
        weave(nc.scalar.copy, y_grp[1], y_rows, 256, NQ)
        quant(v_codes[0][:], v_scales[0][:], v_grp01, 0, 2 * P)
        quant(y_codes[:], y_scales[:], y_grp[0], 0, 256)
        quant(y_codes[:], y_scales[:], y_grp[1], 256, NQ)
        v_grp2 = keep.tile([P, P, PACK], BF16, name="v_grp2", align_bytes=64)
        drain_v(nc.scalar.copy, turned2, v_grp2[:])
        quant(v_codes[1][:], v_scales[1][:], v_grp2, 0, P)
        got3 = gather_v(3, big.tile([P, 4 * N], BF16, name="v_got3", offset=4 * SLOT, align_bytes=64)[:, 0:N])

        out_rows = out[0].rearrange("(j p) e -> p j e", p=P)

        def second_layer(part, e0, width, j0, nj, tag, copy, res):
            acc = psum.tile([P, nj, width], F32, name="acc", tag=tag)
            for j in range(nj):
                rows = slice(P * (j0 + j), P * (j0 + j + 1))
                nc.tensor.matmul_mx(
                    out=acc[:, j, :],
                    lhsT=y_codes[:, rows].bitcast(FP8X4),
                    lhsT_scale=y_scales[:, rows],
                    rhs=v_codes[part][:].bitcast(FP8X4),
                    rhs_scale=v_scales[part][:],
                    start=True,
                    stop=True,
                )
            copy(res[:], acc[:])
            nc.sync.dma_start(out_rows[:, j0 : j0 + nj, e0 : e0 + width], res[:])

        res_a = keep.tile([P, 2, 256], F32, name="res_a")
        second_layer(0, 0, 256, 0, 2, "bank2", nc.scalar.copy, res_a)
        res_b = big.tile([P, 2, 256], F32, name="res_b", offset=6 * SLOT, align_bytes=64)
        second_layer(0, 0, 256, 2, 2, "bank3", nc.vector.tensor_copy, res_b)
        res_c = big.tile([P, 4, 128], F32, name="res_c", offset=6 * SLOT + 2048, align_bytes=64)
        second_layer(1, 256, 128, 0, 4, "bank6", nc.vector.tensor_copy, res_c)
        turned3 = turn_v(3, got3)
        v_grp3 = keep.tile([P, P, PACK], BF16, name="v_grp3", align_bytes=64)
        drain_v(nc.scalar.copy, turned3, v_grp3[:])
        quant(v_codes[2][:], v_scales[2][:], v_grp3, 0, P)
        res_d = keep.tile([P, 2, 128], F32, name="res_d")
        res_e = keep.tile([P, 2, 128], F32, name="res_e")
        second_layer(2, 384, 128, 0, 2, "bank0", nc.scalar.copy, res_d)
        second_layer(2, 384, 128, 2, 2, "bank7", nc.vector.tensor_copy, res_e)
